import numpy as np
import ml_dtypes


def mxq(x, axis, fmt="e4m3"):
    dtype, down = {"e4m3": (ml_dtypes.float8_e4m3fn, 7), "e5m2": (ml_dtypes.float8_e5m2, 14)}[fmt]
    v = np.moveaxis(np.asarray(x, np.float32).astype(ml_dtypes.bfloat16).astype(np.float64), axis, -1)
    blocks = v.reshape(v.shape[:-1] + (-1, 32))
    amax = np.abs(blocks).max(-1, keepdims=True)
    byte = np.maximum(np.where(amax > 0, np.frexp(amax)[1] - 1 + 127, 0) - down, 1)
    scale = np.exp2(byte - 127.0)
    codes = (blocks / scale).astype(np.float32).astype(dtype).astype(np.float64)
    return np.moveaxis((codes * scale).reshape(v.shape), -1, axis)


WIDE = False


def mx_kscale(k):
    if not WIDE:
        return np.ones(k)
    levels = np.array([10, -10, 5, -5, 0])
    if k % 512:
        return np.exp2(np.random.permutation(np.resize(levels, k // 32))).repeat(32)
    a = np.empty((k // 512, 16))
    for p in range(k // 512):
        a[p, :8] = np.random.permutation(np.resize(levels, 8))
        for g in range(8):
            far = levels[np.abs(levels - a[p, g]) >= 10]
            a[p, g + 8] = far[np.random.randint(len(far))]
    return np.exp2(a.ravel()).repeat(32)


def f64(x):
    return np.asarray(x).astype(np.float64)


def striped(idx):
    return np.tile(np.asarray(idx).reshape(-1, 16).T, (8, 1)).astype(np.uint16)


def unstriped(offs):
    return offs[:16].T.reshape(-1).astype(np.int64)


E2M1 = np.array([0.0, 0.5, 1.0, 1.5, 2.0, 3.0, 4.0, 6.0, -0.0, -0.5, -1.0, -1.5, -2.0, -3.0, -4.0, -6.0])


def pack_weight(w, fmt):
    k, n = w.shape
    w = f64(np.asarray(w, np.float32).astype(ml_dtypes.bfloat16)).reshape(k // 32, 32, n)
    amax = np.abs(w).max(1)
    if fmt == "e4m3":
        byte = np.frexp(amax)[1] - 1 + 127 - 7
    else:
        mant, ex = np.frexp(amax / 6.0)
        byte = np.where(mant > 0.5, ex, ex - 1) + 127
    byte = np.clip(np.where(amax > 0, byte, 1), 1, 254)
    scaled = (w * np.exp2(127.0 - byte)[:, None, :]).reshape(k, n).astype(np.float32)
    by_word = np.ascontiguousarray(scaled.reshape(k // 512, 128, 4, n).transpose(0, 1, 3, 2))
    if fmt == "e4m3":
        words = by_word.astype(ml_dtypes.float8_e4m3fn).view(np.uint8)
    else:
        c = by_word.astype(ml_dtypes.float4_e2m1fn).view(np.uint8) & 0xF
        words = (c[..., 0::2] | (c[..., 1::2] << 4)).reshape(k // 512, 128, 2 * n)
    return np.ascontiguousarray(words), np.ascontiguousarray(byte.astype(np.uint8).reshape(k // 512, 16, n))


def unpack_weight(words, scales, fmt):
    g, _, n = scales.shape
    words = np.ascontiguousarray(words).reshape(g, 128, n, -1)
    if fmt == "e4m3":
        vals = words.view(ml_dtypes.float8_e4m3fn).astype(np.float64)
    else:
        nib = np.empty((g, 128, n, 4), np.uint8)
        nib[..., 0::2] = words & 0xF
        nib[..., 1::2] = words >> 4
        vals = E2M1[nib]
    vals = vals * np.repeat(np.exp2(scales.astype(np.float64) - 127.0), 8, axis=1)[..., None]
    return vals.transpose(0, 1, 3, 2).reshape(g * 512, n)


D, T, I, Q, E, Z, M = 512, 2048, 512, 256, 512, 1024, 1024


def setup_inputs():
    n = np.random.standard_normal
    idx = np.random.permutation(T)[:I]
    idx2 = np.random.permutation(Z)[:I]
    idx3 = np.random.permutation(M)[:Q]
    fd = mx_kscale(D)
    fi = mx_kscale(I)
    ti = np.ones(T)
    ti[idx] = fi
    keysp = pack_weight(n((D, T)) / fd[:, None], "e2m1")
    return {
        "query": (n((D, Q)) * 1.0 / np.sqrt(D) * fd[:, None]).astype(np.float32),
        "keys_words": keysp[0],
        "keys_scales": keysp[1],
        "earl": (np.random.uniform(0.3, 1.7, (Q, Z))).astype(np.float32),
        "os": (np.random.uniform(0.02, 0.08, (1, I)) * fi).astype(np.float32),
        "vals": (n((E, T)) / ti).astype(np.float32),
        "old": (n((E, M)) * 2.0).astype(np.float32),
        "fade": (np.random.uniform(0.3, 0.9, (1, M))).astype(np.float32),
        "offs": striped(idx),
        "offs2": striped(idx2),
        "offs3": striped(idx3),
    }


def reference(query, keys_words, keys_scales, earl, os, vals, old, fade, offs, offs2, offs3):
    idx = unstriped(offs)
    idx2 = unstriped(offs2)
    idx3 = unstriped(offs3)
    keysu = unpack_weight(keys_words, keys_scales, "e2m1")
    queryq = mxq(f64(query), 0, "e4m3")
    keysidxg = keysu[:, idx]
    a = queryq.T @ keysidxg
    w = a * f64(earl)[:, idx2]
    wo1 = w * f64(os)
    wt1 = wo1.T
    vt1 = f64(vals)[:, idx].T
    vt1q = mxq(vt1, 0, "e4m3")
    wt1q = mxq(wt1, 0, "e4m3")
    o = vt1q.T @ wt1q
    of = np.zeros((E, M))
    of[:, idx3] = o
    y = f64(old) * f64(fade) + of
    return y

@@ -1,0 +1,208 @@
+from contextlib import ExitStack
+
+import concourse.mybir as mybir
+from concourse.masks import make_identity
+
+D, T, I, Q, E, Z, M = 512, 2048, 512, 256, 512, 1024, 1024
+FLOPS = 2 * D * Q * I + 2 * I * E * Q
+
+F32 = mybir.dt.float32
+BF16 = mybir.dt.bfloat16
+I32 = mybir.dt.int32
+U32 = mybir.dt.uint32
+U16 = mybir.dt.uint16
+U8 = mybir.dt.uint8
+FP8X4 = mybir.dt.float8_e4m3fn_x4
+FP4X4 = mybir.dt.float4_e2m1fn_x4
+MULT = mybir.AluOpType.mult
+ADD = mybir.AluOpType.add
+COPY = mybir.ActivationFunctionType.Copy
+
+P = 128
+PACK = 4
+BANK = 512
+Q_TILES = Q // P
+E_TILES = E // P
+M_HALVES = M // BANK
+
+
+def tile_attend_earliertable_written_lean_kernel(
+    tc, query, keys_words, keys_scales, earl, slot_factor, vals, old, fade, offs, offs2, offs3, out
+):
+    nc = tc.nc
+    with ExitStack() as ctx:
+        keep = ctx.enter_context(tc.tile_pool(name="keep", bufs=1))
+        work = ctx.enter_context(tc.tile_pool(name="work", bufs=4))
+        psum = ctx.enter_context(tc.psum_pool(name="psum", bufs=1))
+        psum2 = ctx.enter_context(tc.psum_pool(name="psum2", bufs=2))
+
+        slots = keep.tile([P, I // 16], U16, name="slots")
+        slots2 = keep.tile([P, I // 16], U16, name="slots2")
+        places = keep.tile([P, Q // 16], U16, name="places")
+        key_words = keep.tile([P, T], U16, name="key_words")
+        key_scales = keep.tile([P, T], U8, name="key_scales")
+        q_raw = keep.tile([P, PACK, Q], F32, name="q_raw")
+        os_col = keep.tile([P, 1, PACK], F32, name="os_col")
+        fade_col = keep.tile([P, M_HALVES * PACK], F32, name="fade_col")
+        earl_sb = [keep.tile([P, Z], F32, name=f"earl{j}") for j in range(Q_TILES)]
+        vals_sb = [keep.tile([P, T], F32, name="vals_sb", tag=f"vals{k}") for k in range(E_TILES)]
+        old_sb = [keep.tile([P, M], F32, name=f"old{k}") for k in range(E_TILES)]
+        placed = [keep.tile([P, M], F32, name=f"placed{k}") for k in range(2)]
+        ident = keep.tile([P, P], F32, name="ident")
+
+        nc.gpsimd.memset(key_scales[:].bitcast(I32), 0)
+        make_identity(nc, ident[:])
+        for window in placed:
+            nc.vector.memset(window[:], 0.0)
+
+        nc.sync.dma_start(slots[:], offs)
+        for quad in range(4):
+            nc.scalar.dma_start(
+                key_scales[32 * quad : 32 * quad + 4, :].bitcast(I32),
+                keys_scales[0, 4 * quad : 4 * quad + 4, :].bitcast(I32),
+            )
+        nc.sync.dma_start(q_raw[:], query.rearrange("(p t) q -> p t q", t=PACK))
+        nc.sync.dma_start(slots2[:], offs2)
+        nc.sync.dma_start(earl_sb[0][:], earl[0:P, :])
+        nc.sync.dma_start(places[:], offs3)
+        nc.sync.dma_start(key_words[:].bitcast(I32), keys_words[0].bitcast(I32))
+        nc.sync.dma_start(earl_sb[1][:], earl[P : 2 * P, :])
+        nc.scalar.dma_start(os_col[:, 0, :], slot_factor[0].rearrange("(p t) -> p t", t=PACK))
+        nc.scalar.dma_start(
+            fade_col[:].rearrange("n (h j) -> n h j", j=PACK),
+            fade[0].rearrange("(h n j) -> n h j", h=M_HALVES, j=PACK),
+        )
+
+        def load_vals(k):
+            nc.sync.dma_start(vals_sb[k][:], vals[k * P : (k + 1) * P, :])
+
+        def load_old(k):
+            nc.sync.dma_start(old_sb[k][:], old[k * P : (k + 1) * P, :])
+
+        load_vals(0)
+        for k in range(1, E_TILES):
+            load_vals(k)
+            load_old(k - 1)
+        load_old(E_TILES - 1)
+
+        k_words = keep.tile([P, I], U16, name="k_words", align_bytes=64)
+        k_scales = keep.tile([P, I], U8, name="k_scales", align_bytes=64)
+        nc.vector.tensor_copy(k_scales[:], key_scales[:].indirect(slots[:]))
+
+        q_bf = keep.tile([P, Q, PACK], BF16, name="q_bf", align_bytes=64)
+        nc.scalar.activation(q_bf[:], q_raw[:].rearrange("p t q -> p q t"), COPY)
+        q_codes = keep.tile([P, Q], U32, name="q_codes", align_bytes=64)
+        q_scales = keep.tile([P, Q], U8, name="q_scales", align_bytes=64)
+        nc.vector.quantize_mx(
+            out=q_codes[:].bitcast(FP8X4), scales=q_scales[:], in_=q_bf[:].rearrange("p q t -> p (q t)")
+        )
+
+        nc.vector.tensor_copy(k_words[:], key_words[:].indirect(slots[:]))
+
+        w_bf = keep.tile([P, Q, PACK], BF16, name="w_bf", align_bytes=64)
+        scores = []
+        earl_g = []
+        for j in range(Q_TILES):
+            a = psum.tile([P, BANK], F32, name="a", tag=f"row{j}")
+            nc.tensor.matmul_mx(
+                out=a[:],
+                lhsT=q_codes[:, j * P : (j + 1) * P].bitcast(FP8X4),
+                lhsT_scale=q_scales[:, j * P : (j + 1) * P],
+                rhs=k_words[:].bitcast(FP4X4),
+                rhs_scale=k_scales[:],
+                start=True,
+                stop=True,
+            )
+            scores.append(a)
+            g = work.tile([P, I], F32, name="earl_g")
+            nc.scalar.activation(g[:], earl_sb[j][:].indirect(slots2[:]), COPY)
+            earl_g.append(g)
+
+        turned = []
+        for j in range(Q_TILES):
+            w = work.tile([P, I], F32, name="w")
+            nc.vector.tensor_tensor(w[:], scores[j][:], earl_g[j][:], MULT)
+            wt = psum.tile([P, PACK, P], F32, name="wt", tag=f"turn{j}")
+            for t in range(PACK):
+                nc.tensor.transpose(wt[:, t, :], w[:, t::PACK], ident[:])
+            turned.append(wt)
+        w_codes = keep.tile([P, Q], U32, name="w_codes", align_bytes=64)
+        w_scales = keep.tile([P, Q], U8, name="w_scales", align_bytes=64)
+        for j in range(Q_TILES):
+            nc.vector.tensor_tensor(
+                w_bf[:, j * P : (j + 1) * P, :],
+                turned[j][:].rearrange("p t q -> p q t"),
+                os_col[:].to_broadcast([P, P, PACK]),
+                MULT,
+            )
+            nc.vector.quantize_mx(
+                out=w_codes[:, j * P : (j + 1) * P].bitcast(FP8X4),
+                scales=w_scales[:, j * P : (j + 1) * P],
+                in_=w_bf[:, j * P : (j + 1) * P, :].rearrange("p q t -> p (q t)"),
+            )
+
+        fade_ps = []
+        for h in range(M_HALVES):
+            f = psum.tile([P, PACK, P], F32, name="fade_rows", tag=f"row{h}")
+            for j in range(PACK):
+                c = h * PACK + j
+                nc.tensor.transpose(f[:, j, :], fade_col[:, c : c + 1].to_broadcast([P, P]), ident[:])
+            fade_ps.append(f)
+
+        def quantise_vals(k):
+            v_bf = keep.tile([P, I], BF16, name="v_bf", tag=("staged0", "staged1", "staged0", "vals2")[k])
+            nc.scalar.activation(v_bf[:], vals_sb[k][:].indirect(slots[:]), COPY)
+            pairs = v_bf[:].bitcast(F32)
+            vt = psum.tile([P, 2, P], F32, name="vt", tag=f"turn{k % 2}")
+            for u in range(2):
+                nc.tensor.transpose(vt[:, u, :], pairs[:, u::2], ident[:])
+            vt_bf = keep.tile([P, P * PACK], BF16, name="vt_bf", align_bytes=64, tag=("result0", "faded", "result1", "result2")[k])
+            nc.vector.tensor_copy(
+                vt_bf[:].bitcast(F32).rearrange("p (e u) -> p e u", u=2), vt[:].rearrange("p u e -> p e u")
+            )
+            v_codes = work.tile([P, P], U32, name="v_codes", align_bytes=64)
+            v_scales = work.tile([P, P], U8, name="v_scales", align_bytes=64)
+            nc.vector.quantize_mx(out=v_codes[:].bitcast(FP8X4), scales=v_scales[:], in_=vt_bf[:])
+            return v_codes, v_scales
+
+        def multiply_and_place(k, v_codes, v_scales):
+            o = psum2.tile([P, BANK], F32, name="o")
+            nc.tensor.matmul_mx(
+                out=o[:, 0:Q],
+                lhsT=v_codes[:].bitcast(FP8X4),
+                lhsT_scale=v_scales[:],
+                rhs=w_codes[:].bitcast(FP8X4),
+                rhs_scale=w_scales[:],
+                start=True,
+                stop=True,
+            )
+            o_sb = keep.tile([P, Q], F32, name="o_sb", tag=("staged0", "vals2", "vals3", "staged1")[k])
+            nc.scalar.copy(o_sb[:], o[:, 0:Q])
+            nc.scalar.activation(placed[k % 2][:].indirect(places[:]), o_sb[:], COPY)
+
+        def fade_old(k):
+            faded = keep.tile([P, M], F32, name="faded", align_bytes=64, tag="faded")
+            for h in range(M_HALVES):
+                cols = slice(h * BANK, (h + 1) * BANK)
+                nc.vector.tensor_tensor(
+                    faded[:, cols].rearrange("p (n j) -> p n j", j=PACK),
+                    old_sb[k][:, cols].rearrange("p (n j) -> p n j", j=PACK),
+                    fade_ps[h][:].rearrange("p j n -> p n j"),
+                    MULT,
+                )
+            return faded
+
+        def finish(k, faded):
+            result = keep.tile([P, M], F32, name="result", align_bytes=64, tag=f"result{k}")
+            pieces = 2 if k == E_TILES - 1 else 1
+            for h in range(pieces):
+                cols = slice(h * M // pieces, (h + 1) * M // pieces)
+                nc.vector.tensor_tensor(result[:, cols], faded[:, cols], placed[k % 2][:, cols], ADD)
+                nc.sync.dma_start(out[k * P : (k + 1) * P, cols], result[:, cols])
+
+        quantised = [quantise_vals(0), quantise_vals(1)]
+        for k in range(E_TILES):
+            multiply_and_place(k, *quantised[k])
+            if k + 2 < E_TILES:
+                quantised.append(quantise_vals(k + 2))
+            finish(k, fade_old(k))

@@ -42,11 +42,11 @@ def tile_attend_earliertable_written_lean_kernel(
         key_words = keep.tile([P, T], U16, name="key_words")
         key_scales = keep.tile([P, T], U8, name="key_scales")
         q_raw = keep.tile([P, PACK, Q], F32, name="q_raw")
-        os_col = keep.tile([P, 1, PACK], F32, name="os_col")
+        os_col = keep.tile([P, 1, PACK], F32, name="os_col", align_bytes=64, tag="factor")
         fade_col = keep.tile([P, M_HALVES * PACK], F32, name="fade_col")
         earl_sb = [keep.tile([P, Z], F32, name=f"earl{j}") for j in range(Q_TILES)]
-        vals_sb = [keep.tile([P, T], F32, name="vals_sb", tag=f"vals{k}") for k in range(E_TILES)]
-        old_sb = [keep.tile([P, M], F32, name=f"old{k}") for k in range(E_TILES)]
+        vals_sb = [keep.tile([P, T], F32, name="vals_sb", align_bytes=64, tag=f"vals{k}") for k in range(E_TILES)]
+        old_sb = [keep.tile([P, M], F32, name="old_sb", align_bytes=64, tag=f"old{k}") for k in range(E_TILES)]
         placed = [keep.tile([P, M], F32, name=f"placed{k}") for k in range(2)]
         ident = keep.tile([P, P], F32, name="ident")
 
@@ -64,11 +64,10 @@ def tile_attend_earliertable_written_lean_kernel(
         nc.sync.dma_start(q_raw[:], query.rearrange("(p t) q -> p t q", t=PACK))
         nc.sync.dma_start(slots2[:], offs2)
         nc.sync.dma_start(earl_sb[0][:], earl[0:P, :])
-        nc.sync.dma_start(places[:], offs3)
         nc.sync.dma_start(key_words[:].bitcast(I32), keys_words[0].bitcast(I32))
         nc.sync.dma_start(earl_sb[1][:], earl[P : 2 * P, :])
-        nc.scalar.dma_start(os_col[:, 0, :], slot_factor[0].rearrange("(p t) -> p t", t=PACK))
-        nc.scalar.dma_start(
+        nc.gpsimd.dma_start(os_col[:, 0, :], slot_factor[0].rearrange("(p t) -> p t", t=PACK))
+        nc.gpsimd.dma_start(
             fade_col[:].rearrange("n (h j) -> n h j", j=PACK),
             fade[0].rearrange("(h n j) -> n h j", h=M_HALVES, j=PACK),
         )
@@ -82,15 +81,25 @@ def tile_attend_earliertable_written_lean_kernel(
         load_vals(0)
         for k in range(1, E_TILES):
             load_vals(k)
+            if k == 1:
+                nc.sync.dma_start(places[:], offs3)
             load_old(k - 1)
         load_old(E_TILES - 1)
+
+        fade_ps = []
+        for h in range(M_HALVES):
+            f = psum.tile([P, PACK, P], F32, name="fade_rows", tag=f"fade{h}")
+            for j in range(PACK):
+                c = h * PACK + j
+                nc.tensor.transpose(f[:, j, :], fade_col[:, c : c + 1].to_broadcast([P, P]), ident[:])
+            fade_ps.append(f)
 
         k_words = keep.tile([P, I], U16, name="k_words", align_bytes=64)
         k_scales = keep.tile([P, I], U8, name="k_scales", align_bytes=64)
         nc.vector.tensor_copy(k_scales[:], key_scales[:].indirect(slots[:]))
 
         q_bf = keep.tile([P, Q, PACK], BF16, name="q_bf", align_bytes=64)
-        nc.scalar.activation(q_bf[:], q_raw[:].rearrange("p t q -> p q t"), COPY)
+        nc.vector.tensor_copy(q_bf[:], q_raw[:].rearrange("p t q -> p q t"))
         q_codes = keep.tile([P, Q], U32, name="q_codes", align_bytes=64)
         q_scales = keep.tile([P, Q], U8, name="q_scales", align_bytes=64)
         nc.vector.quantize_mx(
@@ -141,22 +150,17 @@ def tile_attend_earliertable_written_lean_kernel(
                 in_=w_bf[:, j * P : (j + 1) * P, :].rearrange("p q t -> p (q t)"),
             )
 
-        fade_ps = []
-        for h in range(M_HALVES):
-            f = psum.tile([P, PACK, P], F32, name="fade_rows", tag=f"row{h}")
-            for j in range(PACK):
-                c = h * PACK + j
-                nc.tensor.transpose(f[:, j, :], fade_col[:, c : c + 1].to_broadcast([P, P]), ident[:])
-            fade_ps.append(f)
-
         def quantise_vals(k):
-            v_bf = keep.tile([P, I], BF16, name="v_bf", tag=("staged0", "staged1", "staged0", "vals2")[k])
-            nc.scalar.activation(v_bf[:], vals_sb[k][:].indirect(slots[:]), COPY)
+            v_bf = work.tile([P, I], BF16, name="v_bf")
+            if k == 2:
+                nc.vector.tensor_copy(v_bf[:], vals_sb[k][:].indirect(slots[:]))
+            else:
+                nc.scalar.activation(v_bf[:], vals_sb[k][:].indirect(slots[:]), COPY)
             pairs = v_bf[:].bitcast(F32)
             vt = psum.tile([P, 2, P], F32, name="vt", tag=f"turn{k % 2}")
             for u in range(2):
                 nc.tensor.transpose(vt[:, u, :], pairs[:, u::2], ident[:])
-            vt_bf = keep.tile([P, P * PACK], BF16, name="vt_bf", align_bytes=64, tag=("result0", "faded", "result1", "result2")[k])
+            vt_bf = keep.tile([P, P * PACK], BF16, name="vt_bf", align_bytes=64, tag=("factor", "old0", "vt_bf2", "vt_bf3")[k])
             nc.vector.tensor_copy(
                 vt_bf[:].bitcast(F32).rearrange("p (e u) -> p e u", u=2), vt[:].rearrange("p u e -> p e u")
             )
@@ -176,12 +180,12 @@ def tile_attend_earliertable_written_lean_kernel(
                 start=True,
                 stop=True,
             )
-            o_sb = keep.tile([P, Q], F32, name="o_sb", tag=("staged0", "vals2", "vals3", "staged1")[k])
+            o_sb = keep.tile([P, Q], F32, name="o_sb", align_bytes=64, tag=("vals1", "o_sb1", "vals3", "o_sb3")[k])
             nc.scalar.copy(o_sb[:], o[:, 0:Q])
             nc.scalar.activation(placed[k % 2][:].indirect(places[:]), o_sb[:], COPY)
 
         def fade_old(k):
-            faded = keep.tile([P, M], F32, name="faded", align_bytes=64, tag="faded")
+            faded = keep.tile([P, M], F32, name="faded", tag=f"faded{k}")
             for h in range(M_HALVES):
                 cols = slice(h * BANK, (h + 1) * BANK)
                 nc.vector.tensor_tensor(
@@ -193,16 +197,24 @@ def tile_attend_earliertable_written_lean_kernel(
             return faded
 
         def finish(k, faded):
-            result = keep.tile([P, M], F32, name="result", align_bytes=64, tag=f"result{k}")
+            result = keep.tile([P, M], F32, name="result", align_bytes=64, tag="vals2" if k == 0 else f"result{k}")
             pieces = 2 if k == E_TILES - 1 else 1
             for h in range(pieces):
                 cols = slice(h * M // pieces, (h + 1) * M // pieces)
                 nc.vector.tensor_tensor(result[:, cols], faded[:, cols], placed[k % 2][:, cols], ADD)
                 nc.sync.dma_start(out[k * P : (k + 1) * P, cols], result[:, cols])
 
-        quantised = [quantise_vals(0), quantise_vals(1)]
-        for k in range(E_TILES):
-            multiply_and_place(k, *quantised[k])
-            if k + 2 < E_TILES:
-                quantised.append(quantise_vals(k + 2))
-            finish(k, fade_old(k))
+        first = quantise_vals(0)
+        multiply_and_place_later = [first]
+        faded = [fade_old(0)]
+        multiply_and_place_later.append(quantise_vals(1))
+        multiply_and_place(0, *multiply_and_place_later[0])
+        third = quantise_vals(2)
+        finish(0, faded[0])
+        multiply_and_place(1, *multiply_and_place_later[1])
+        finish(1, fade_old(1))
+        fourth = quantise_vals(3)
+        multiply_and_place(2, *third)
+        finish(2, fade_old(2))
+        multiply_and_place(3, *fourth)
+        finish(3, fade_old(3))

@@ -55,43 +55,43 @@ def tile_attend_earliertable_written_lean_kernel(
         for window in placed:
             nc.vector.memset(window[:], 0.0)
 
-        nc.sync.dma_start(slots[:], offs)
-        for quad in range(4):
-            nc.scalar.dma_start(
-                key_scales[32 * quad : 32 * quad + 4, :].bitcast(I32),
-                keys_scales[0, 4 * quad : 4 * quad + 4, :].bitcast(I32),
-            )
-        nc.sync.dma_start(q_raw[:], query.rearrange("(p t) q -> p t q", t=PACK))
-        nc.sync.dma_start(slots2[:], offs2)
-        nc.sync.dma_start(earl_sb[0][:], earl[0:P, :])
-        nc.sync.dma_start(key_words[:].bitcast(I32), keys_words[0].bitcast(I32))
-        nc.sync.dma_start(earl_sb[1][:], earl[P : 2 * P, :])
-        nc.gpsimd.dma_start(os_col[:, 0, :], slot_factor[0].rearrange("(p t) -> p t", t=PACK))
-        nc.gpsimd.dma_start(
-            fade_col[:].rearrange("n (h j) -> n h j", j=PACK),
-            fade[0].rearrange("(h n j) -> n h j", h=M_HALVES, j=PACK),
-        )
-
         def load_vals(k):
             nc.sync.dma_start(vals_sb[k][:], vals[k * P : (k + 1) * P, :])
 
         def load_old(k):
             nc.sync.dma_start(old_sb[k][:], old[k * P : (k + 1) * P, :])
 
+        nc.sync.dma_start(slots[:], offs)
+        nc.sync.dma_start(slots2[:], offs2)
+        nc.sync.dma_start(q_raw[:], query.rearrange("(p t) q -> p t q", t=PACK))
+        nc.sync.dma_start(earl_sb[0][:], earl[0:P, :])
+        for quad in range(4):
+            nc.sync.dma_start(
+                key_scales[32 * quad : 32 * quad + 4, :].bitcast(I32),
+                keys_scales[0, 4 * quad : 4 * quad + 4, :].bitcast(I32),
+            )
+        nc.sync.dma_start(key_words[:].bitcast(I32), keys_words[0].bitcast(I32))
+        nc.sync.dma_start(earl_sb[1][:], earl[P : 2 * P, :])
+        nc.sync.dma_start(os_col[:, 0, :], slot_factor[0].rearrange("(p t) -> p t", t=PACK))
         load_vals(0)
-        for k in range(1, E_TILES):
+        nc.sync.dma_start(
+            fade_col[:].rearrange("n (h j) -> n h j", j=PACK),
+            fade[0].rearrange("(h n j) -> n h j", h=M_HALVES, j=PACK),
+        )
+        load_vals(1)
+        nc.sync.dma_start(places[:], offs3)
+        load_old(0)
+        for k in range(2, E_TILES):
             load_vals(k)
-            if k == 1:
-                nc.sync.dma_start(places[:], offs3)
             load_old(k - 1)
         load_old(E_TILES - 1)
 
         fade_ps = []
         for h in range(M_HALVES):
-            f = psum.tile([P, PACK, P], F32, name="fade_rows", tag=f"fade{h}")
+            f = psum.tile([P, BANK], F32, name="fade_rows", tag=f"fade{h}")
             for j in range(PACK):
                 c = h * PACK + j
-                nc.tensor.transpose(f[:, j, :], fade_col[:, c : c + 1].to_broadcast([P, P]), ident[:])
+                nc.tensor.transpose(f[:, j::PACK], fade_col[:, c : c + 1].to_broadcast([P, P]), ident[:])
             fade_ps.append(f)
 
         k_words = keep.tile([P, I], U16, name="k_words", align_bytes=64)
@@ -99,7 +99,7 @@ def tile_attend_earliertable_written_lean_kernel(
         nc.vector.tensor_copy(k_scales[:], key_scales[:].indirect(slots[:]))
 
         q_bf = keep.tile([P, Q, PACK], BF16, name="q_bf", align_bytes=64)
-        nc.vector.tensor_copy(q_bf[:], q_raw[:].rearrange("p t q -> p q t"))
+        nc.scalar.activation(q_bf[:], q_raw[:].rearrange("p t q -> p q t"), COPY)
         q_codes = keep.tile([P, Q], U32, name="q_codes", align_bytes=64)
         q_scales = keep.tile([P, Q], U8, name="q_scales", align_bytes=64)
         nc.vector.quantize_mx(
@@ -189,9 +189,9 @@ def tile_attend_earliertable_written_lean_kernel(
             for h in range(M_HALVES):
                 cols = slice(h * BANK, (h + 1) * BANK)
                 nc.vector.tensor_tensor(
-                    faded[:, cols].rearrange("p (n j) -> p n j", j=PACK),
-                    old_sb[k][:, cols].rearrange("p (n j) -> p n j", j=PACK),
-                    fade_ps[h][:].rearrange("p j n -> p n j"),
+                    faded[:, cols],
+                    old_sb[k][:, cols],
+                    fade_ps[h][:],
                     MULT,
                 )
             return faded

@@ -62,7 +62,10 @@ def tile_attend_earliertable_written_lean_kernel(
             nc.sync.dma_start(old_sb[k][:], old[k * P : (k + 1) * P, :])
 
         nc.sync.dma_start(slots[:], offs)
-        nc.sync.dma_start(slots2[:], offs2)
+        nc.sync.dma_start(
+            fade_col[:].rearrange("n (h j) -> n h j", j=PACK),
+            fade[0].rearrange("(h n j) -> n h j", h=M_HALVES, j=PACK),
+        )
         nc.sync.dma_start(q_raw[:], query.rearrange("(p t) q -> p t q", t=PACK))
         nc.sync.dma_start(earl_sb[0][:], earl[0:P, :])
         for quad in range(4):
@@ -71,13 +74,10 @@ def tile_attend_earliertable_written_lean_kernel(
                 keys_scales[0, 4 * quad : 4 * quad + 4, :].bitcast(I32),
             )
         nc.sync.dma_start(key_words[:].bitcast(I32), keys_words[0].bitcast(I32))
+        nc.sync.dma_start(slots2[:], offs2)
         nc.sync.dma_start(earl_sb[1][:], earl[P : 2 * P, :])
         nc.sync.dma_start(os_col[:, 0, :], slot_factor[0].rearrange("(p t) -> p t", t=PACK))
         load_vals(0)
-        nc.sync.dma_start(
-            fade_col[:].rearrange("n (h j) -> n h j", j=PACK),
-            fade[0].rearrange("(h n j) -> n h j", h=M_HALVES, j=PACK),
-        )
         load_vals(1)
         nc.sync.dma_start(places[:], offs3)
         load_old(0)
@@ -130,10 +130,15 @@ def tile_attend_earliertable_written_lean_kernel(
         turned = []
         for j in range(Q_TILES):
             w = work.tile([P, I], F32, name="w")
-            nc.vector.tensor_tensor(w[:], scores[j][:], earl_g[j][:], MULT)
+            nc.vector.tensor_tensor(
+                w[:].rearrange("p (t c i) -> p c t i", t=PACK, i=PACK),
+                scores[j][:].rearrange("p (c i t) -> p c t i", t=PACK, i=PACK),
+                earl_g[j][:].rearrange("p (c i t) -> p c t i", t=PACK, i=PACK),
+                MULT,
+            )
             wt = psum.tile([P, PACK, P], F32, name="wt", tag=f"turn{j}")
             for t in range(PACK):
-                nc.tensor.transpose(wt[:, t, :], w[:, t::PACK], ident[:])
+                nc.tensor.transpose(wt[:, t, :], w[:, t * P : (t + 1) * P], ident[:])
             turned.append(wt)
         w_codes = keep.tile([P, Q], U32, name="w_codes", align_bytes=64)
         w_scales = keep.tile([P, Q], U8, name="w_scales", align_bytes=64)

@@ -42,7 +42,7 @@ def tile_attend_earliertable_written_lean_kernel(
         key_words = keep.tile([P, T], U16, name="key_words")
         key_scales = keep.tile([P, T], U8, name="key_scales")
         q_raw = keep.tile([P, PACK, Q], F32, name="q_raw")
-        os_col = keep.tile([P, 1, PACK], F32, name="os_col", align_bytes=64, tag="factor")
+        os_col = keep.tile([P, 1, PACK], F32, name="os_col")
         fade_col = keep.tile([P, M_HALVES * PACK], F32, name="fade_col")
         earl_sb = [keep.tile([P, Z], F32, name=f"earl{j}") for j in range(Q_TILES)]
         vals_sb = [keep.tile([P, T], F32, name="vals_sb", align_bytes=64, tag=f"vals{k}") for k in range(E_TILES)]
@@ -62,17 +62,11 @@ def tile_attend_earliertable_written_lean_kernel(
             nc.sync.dma_start(old_sb[k][:], old[k * P : (k + 1) * P, :])
 
         nc.sync.dma_start(slots[:], offs)
-        nc.sync.dma_start(
-            fade_col[:].rearrange("n (h j) -> n h j", j=PACK),
-            fade[0].rearrange("(h n j) -> n h j", h=M_HALVES, j=PACK),
-        )
+        nc.sync.dma_start(fade_col[:], fade[0].rearrange("(n c) -> n c", n=P))
         nc.sync.dma_start(q_raw[:], query.rearrange("(p t) q -> p t q", t=PACK))
         nc.sync.dma_start(earl_sb[0][:], earl[0:P, :])
-        for quad in range(4):
-            nc.sync.dma_start(
-                key_scales[32 * quad : 32 * quad + 4, :].bitcast(I32),
-                keys_scales[0, 4 * quad : 4 * quad + 4, :].bitcast(I32),
-            )
+        for r in range(4):
+            nc.sync.dma_start(key_scales[r:P:32, :].bitcast(I32), keys_scales[0, r:16:4, :].bitcast(I32))
         nc.sync.dma_start(key_words[:].bitcast(I32), keys_words[0].bitcast(I32))
         nc.sync.dma_start(slots2[:], offs2)
         nc.sync.dma_start(earl_sb[1][:], earl[P : 2 * P, :])
@@ -149,27 +143,29 @@ def tile_attend_earliertable_written_lean_kernel(
                 os_col[:].to_broadcast([P, P, PACK]),
                 MULT,
             )
-            nc.vector.quantize_mx(
-                out=w_codes[:, j * P : (j + 1) * P].bitcast(FP8X4),
-                scales=w_scales[:, j * P : (j + 1) * P],
-                in_=w_bf[:, j * P : (j + 1) * P, :].rearrange("p q t -> p (q t)"),
-            )
+        nc.vector.quantize_mx(
+            out=w_codes[:].bitcast(FP8X4), scales=w_scales[:], in_=w_bf[:].rearrange("p q t -> p (q t)")
+        )
 
-        def quantise_vals(k):
+        def gather_vals(k):
             v_bf = work.tile([P, I], BF16, name="v_bf")
             if k == 2:
                 nc.vector.tensor_copy(v_bf[:], vals_sb[k][:].indirect(slots[:]))
             else:
                 nc.scalar.activation(v_bf[:], vals_sb[k][:].indirect(slots[:]), COPY)
+            return v_bf
+
+        def quantise_vals(k, v_bf):
             pairs = v_bf[:].bitcast(F32)
             vt = psum.tile([P, 2, P], F32, name="vt", tag=f"turn{k % 2}")
             for u in range(2):
                 nc.tensor.transpose(vt[:, u, :], pairs[:, u::2], ident[:])
-            vt_bf = keep.tile([P, P * PACK], BF16, name="vt_bf", align_bytes=64, tag=("factor", "old0", "vt_bf2", "vt_bf3")[k])
-            nc.vector.tensor_copy(
+            vt_bf = keep.tile([P, P * PACK], BF16, name="vt_bf", align_bytes=64, tag=("vt_bf0", "old0", "vt_bf2", "vt_bf3")[k])
+            copy = nc.scalar.copy if k % 2 == 0 else nc.vector.tensor_copy
+            copy(
                 vt_bf[:].bitcast(F32).rearrange("p (e u) -> p e u", u=2), vt[:].rearrange("p u e -> p e u")
             )
-            v_codes = work.tile([P, P], U32, name="v_codes", align_bytes=64)
+            v_codes = keep.tile([P, P], U32, name="v_codes", align_bytes=64, tag="old1" if k == 2 else f"codes{k}")
             v_scales = work.tile([P, P], U8, name="v_scales", align_bytes=64)
             nc.vector.quantize_mx(out=v_codes[:].bitcast(FP8X4), scales=v_scales[:], in_=vt_bf[:])
             return v_codes, v_scales
@@ -192,11 +188,10 @@ def tile_attend_earliertable_written_lean_kernel(
         def fade_old(k):
             faded = keep.tile([P, M], F32, name="faded", tag=f"faded{k}")
             for h in range(M_HALVES):
-                cols = slice(h * BANK, (h + 1) * BANK)
                 nc.vector.tensor_tensor(
-                    faded[:, cols],
-                    old_sb[k][:, cols],
-                    fade_ps[h][:],
+                    faded[:].rearrange("p (n h j) -> p h n j", h=M_HALVES, j=PACK)[:, h],
+                    old_sb[k][:].rearrange("p (n h j) -> p h n j", h=M_HALVES, j=PACK)[:, h],
+                    fade_ps[h][:].rearrange("p (n j) -> p n j", j=PACK),
                     MULT,
                 )
             return faded
@@ -209,17 +204,17 @@ def tile_attend_earliertable_written_lean_kernel(
                 nc.vector.tensor_tensor(result[:, cols], faded[:, cols], placed[k % 2][:, cols], ADD)
                 nc.sync.dma_start(out[k * P : (k + 1) * P, cols], result[:, cols])
 
-        first = quantise_vals(0)
-        multiply_and_place_later = [first]
+        quantised = [quantise_vals(0, gather_vals(0))]
         faded = [fade_old(0)]
-        multiply_and_place_later.append(quantise_vals(1))
-        multiply_and_place(0, *multiply_and_place_later[0])
-        third = quantise_vals(2)
+        quantised.append(quantise_vals(1, gather_vals(1)))
+        multiply_and_place(0, *quantised[0])
+        third = gather_vals(2)
         finish(0, faded[0])
-        multiply_and_place(1, *multiply_and_place_later[1])
-        finish(1, fade_old(1))
-        fourth = quantise_vals(3)
-        multiply_and_place(2, *third)
-        finish(2, fade_old(2))
-        multiply_and_place(3, *fourth)
-        finish(3, fade_old(3))
+        multiply_and_place(1, *quantised[1])
+        faded.append(fade_old(1))
+        quantised.append(quantise_vals(2, third))
+        finish(1, faded[1])
+        quantised.append(quantise_vals(3, gather_vals(3)))
+        for k in (2, 3):
+            multiply_and_place(k, *quantised[k])
+            finish(k, fade_old(k))

from contextlib import ExitStack

import concourse.mybir as mybir
from concourse.masks import make_identity

D, T, I, Q, E, Z, M = 512, 2048, 512, 256, 512, 1024, 1024
FLOPS = 2 * D * Q * I + 2 * I * E * Q

F32 = mybir.dt.float32
BF16 = mybir.dt.bfloat16
I32 = mybir.dt.int32
U32 = mybir.dt.uint32
U16 = mybir.dt.uint16
U8 = mybir.dt.uint8
FP8X4 = mybir.dt.float8_e4m3fn_x4
FP4X4 = mybir.dt.float4_e2m1fn_x4
MULT = mybir.AluOpType.mult
ADD = mybir.AluOpType.add
COPY = mybir.ActivationFunctionType.Copy

P = 128
PACK = 4
BANK = 512
Q_TILES = Q // P
E_TILES = E // P
M_HALVES = M // BANK


def tile_attend_earliertable_written_lean_kernel(
    tc, query, keys_words, keys_scales, earl, slot_factor, vals, old, fade, offs, offs2, offs3, out
):
    nc = tc.nc
    with ExitStack() as ctx:
        keep = ctx.enter_context(tc.tile_pool(name="keep", bufs=1))
        work = ctx.enter_context(tc.tile_pool(name="work", bufs=4))
        psum = ctx.enter_context(tc.psum_pool(name="psum", bufs=1))
        psum2 = ctx.enter_context(tc.psum_pool(name="psum2", bufs=2))

        slots = keep.tile([P, I // 16], U16, name="slots")
        slots2 = keep.tile([P, I // 16], U16, name="slots2")
        places = keep.tile([P, Q // 16], U16, name="places")
        key_words = keep.tile([P, T], U16, name="key_words")
        key_scales = keep.tile([P, T], U8, name="key_scales")
        q_raw = keep.tile([P, PACK, Q], F32, name="q_raw")
        os_col = keep.tile([P, 1, PACK], F32, name="os_col")
        fade_col = keep.tile([P, M_HALVES * PACK], F32, name="fade_col")
        earl_sb = [keep.tile([P, Z], F32, name=f"earl{j}") for j in range(Q_TILES)]
        vals_sb = [keep.tile([P, T], F32, name="vals_sb", align_bytes=64, tag=f"vals{k}") for k in range(E_TILES)]
        old_sb = [keep.tile([P, M], F32, name="old_sb", align_bytes=64, tag=f"old{k}") for k in range(E_TILES)]
        placed = [keep.tile([P, M], F32, name=f"placed{k}") for k in range(2)]
        ident = keep.tile([P, P], F32, name="ident")

        nc.gpsimd.memset(key_scales[:].bitcast(I32), 0)
        make_identity(nc, ident[:])
        for window in placed:
            nc.vector.memset(window[:], 0.0)

        def load_vals(k):
            nc.sync.dma_start(vals_sb[k][:], vals[k * P : (k + 1) * P, :])

        def load_old(k):
            nc.sync.dma_start(old_sb[k][:], old[k * P : (k + 1) * P, :])

        nc.sync.dma_start(slots[:], offs)
        nc.sync.dma_start(fade_col[:], fade[0].rearrange("(n c) -> n c", n=P))
        nc.sync.dma_start(q_raw[:], query.rearrange("(p t) q -> p t q", t=PACK))
        nc.sync.dma_start(earl_sb[0][:], earl[0:P, :])
        for r in range(4):
            nc.sync.dma_start(key_scales[r:P:32, :].bitcast(I32), keys_scales[0, r:16:4, :].bitcast(I32))
        nc.sync.dma_start(key_words[:].bitcast(I32), keys_words[0].bitcast(I32))
        nc.sync.dma_start(slots2[:], offs2)
        nc.sync.dma_start(earl_sb[1][:], earl[P : 2 * P, :])
        nc.sync.dma_start(os_col[:, 0, :], slot_factor[0].rearrange("(p t) -> p t", t=PACK))
        load_vals(0)
        load_vals(1)
        nc.sync.dma_start(places[:], offs3)
        load_old(0)
        for k in range(2, E_TILES):
            load_vals(k)
            load_old(k - 1)
        load_old(E_TILES - 1)

        fade_ps = []
        for h in range(M_HALVES):
            f = psum.tile([P, BANK], F32, name="fade_rows", tag=f"fade{h}")
            for j in range(PACK):
                c = h * PACK + j
                nc.tensor.transpose(f[:, j::PACK], fade_col[:, c : c + 1].to_broadcast([P, P]), ident[:])
            fade_ps.append(f)

        k_words = keep.tile([P, I], U16, name="k_words", align_bytes=64)
        k_scales = keep.tile([P, I], U8, name="k_scales", align_bytes=64)
        nc.vector.tensor_copy(k_scales[:], key_scales[:].indirect(slots[:]))

        q_bf = keep.tile([P, Q, PACK], BF16, name="q_bf", align_bytes=64)
        nc.scalar.activation(q_bf[:], q_raw[:].rearrange("p t q -> p q t"), COPY)
        q_codes = keep.tile([P, Q], U32, name="q_codes", align_bytes=64)
        q_scales = keep.tile([P, Q], U8, name="q_scales", align_bytes=64)
        nc.vector.quantize_mx(
            out=q_codes[:].bitcast(FP8X4), scales=q_scales[:], in_=q_bf[:].rearrange("p q t -> p (q t)")
        )

        nc.vector.tensor_copy(k_words[:], key_words[:].indirect(slots[:]))

        w_bf = keep.tile([P, Q, PACK], BF16, name="w_bf", align_bytes=64)
        scores = []
        earl_g = []
        for j in range(Q_TILES):
            a = psum.tile([P, BANK], F32, name="a", tag=f"row{j}")
            nc.tensor.matmul_mx(
                out=a[:],
                lhsT=q_codes[:, j * P : (j + 1) * P].bitcast(FP8X4),
                lhsT_scale=q_scales[:, j * P : (j + 1) * P],
                rhs=k_words[:].bitcast(FP4X4),
                rhs_scale=k_scales[:],
                start=True,
                stop=True,
            )
            scores.append(a)
            g = work.tile([P, I], F32, name="earl_g")
            nc.scalar.activation(g[:], earl_sb[j][:].indirect(slots2[:]), COPY)
            earl_g.append(g)

        turned = []
        for j in range(Q_TILES):
            w = work.tile([P, I], F32, name="w")
            nc.vector.tensor_tensor(
                w[:].rearrange("p (t c i) -> p c t i", t=PACK, i=PACK),
                scores[j][:].rearrange("p (c i t) -> p c t i", t=PACK, i=PACK),
                earl_g[j][:].rearrange("p (c i t) -> p c t i", t=PACK, i=PACK),
                MULT,
            )
            wt = psum.tile([P, PACK, P], F32, name="wt", tag=f"turn{j}")
            for t in range(PACK):
                nc.tensor.transpose(wt[:, t, :], w[:, t * P : (t + 1) * P], ident[:])
            turned.append(wt)
        w_codes = keep.tile([P, Q], U32, name="w_codes", align_bytes=64)
        w_scales = keep.tile([P, Q], U8, name="w_scales", align_bytes=64)
        for j in range(Q_TILES):
            nc.vector.tensor_tensor(
                w_bf[:, j * P : (j + 1) * P, :],
                turned[j][:].rearrange("p t q -> p q t"),
                os_col[:].to_broadcast([P, P, PACK]),
                MULT,
            )
        nc.vector.quantize_mx(
            out=w_codes[:].bitcast(FP8X4), scales=w_scales[:], in_=w_bf[:].rearrange("p q t -> p (q t)")
        )

        def gather_vals(k):
            v_bf = work.tile([P, I], BF16, name="v_bf")
            if k == 2:
                nc.vector.tensor_copy(v_bf[:], vals_sb[k][:].indirect(slots[:]))
            else:
                nc.scalar.activation(v_bf[:], vals_sb[k][:].indirect(slots[:]), COPY)
            return v_bf

        def quantise_vals(k, v_bf):
            pairs = v_bf[:].bitcast(F32)
            vt = psum.tile([P, 2, P], F32, name="vt", tag=f"turn{k % 2}")
            for u in range(2):
                nc.tensor.transpose(vt[:, u, :], pairs[:, u::2], ident[:])
            vt_bf = keep.tile([P, P * PACK], BF16, name="vt_bf", align_bytes=64, tag=("vt_bf0", "old0", "vt_bf2", "vt_bf3")[k])
            copy = nc.scalar.copy if k % 2 == 0 else nc.vector.tensor_copy
            copy(
                vt_bf[:].bitcast(F32).rearrange("p (e u) -> p e u", u=2), vt[:].rearrange("p u e -> p e u")
            )
            v_codes = keep.tile([P, P], U32, name="v_codes", align_bytes=64, tag="old1" if k == 2 else f"codes{k}")
            v_scales = work.tile([P, P], U8, name="v_scales", align_bytes=64)
            nc.vector.quantize_mx(out=v_codes[:].bitcast(FP8X4), scales=v_scales[:], in_=vt_bf[:])
            return v_codes, v_scales

        def multiply_and_place(k, v_codes, v_scales):
            o = psum2.tile([P, BANK], F32, name="o")
            nc.tensor.matmul_mx(
                out=o[:, 0:Q],
                lhsT=v_codes[:].bitcast(FP8X4),
                lhsT_scale=v_scales[:],
                rhs=w_codes[:].bitcast(FP8X4),
                rhs_scale=w_scales[:],
                start=True,
                stop=True,
            )
            o_sb = keep.tile([P, Q], F32, name="o_sb", align_bytes=64, tag=("vals1", "o_sb1", "vals3", "o_sb3")[k])
            nc.scalar.copy(o_sb[:], o[:, 0:Q])
            nc.scalar.activation(placed[k % 2][:].indirect(places[:]), o_sb[:], COPY)

        def fade_old(k):
            faded = keep.tile([P, M], F32, name="faded", tag=f"faded{k}")
            for h in range(M_HALVES):
                nc.vector.tensor_tensor(
                    faded[:].rearrange("p (n h j) -> p h n j", h=M_HALVES, j=PACK)[:, h],
                    old_sb[k][:].rearrange("p (n h j) -> p h n j", h=M_HALVES, j=PACK)[:, h],
                    fade_ps[h][:].rearrange("p (n j) -> p n j", j=PACK),
                    MULT,
                )
            return faded

        def finish(k, faded):
            result = keep.tile([P, M], F32, name="result", align_bytes=64, tag="vals2" if k == 0 else f"result{k}")
            pieces = 2 if k == E_TILES - 1 else 1
            for h in range(pieces):
                cols = slice(h * M // pieces, (h + 1) * M // pieces)
                nc.vector.tensor_tensor(result[:, cols], faded[:, cols], placed[k % 2][:, cols], ADD)
                nc.sync.dma_start(out[k * P : (k + 1) * P, cols], result[:, cols])

        quantised = [quantise_vals(0, gather_vals(0))]
        faded = [fade_old(0)]
        quantised.append(quantise_vals(1, gather_vals(1)))
        multiply_and_place(0, *quantised[0])
        third = gather_vals(2)
        finish(0, faded[0])
        multiply_and_place(1, *quantised[1])
        faded.append(fade_old(1))
        quantised.append(quantise_vals(2, third))
        finish(1, faded[1])
        quantised.append(quantise_vals(3, gather_vals(3)))
        for k in (2, 3):
            multiply_and_place(k, *quantised[k])
            finish(k, fade_old(k))
